import numpy as np, ml_dtypes
CORES = [23,119,17,113]
N = 4
BF = ml_dtypes.bfloat16
NN, P, LN, RO = 512, 2, 256, 6
W = 8 * NN
ACT = (P * np.arange(LN)[None, :] + np.arange(RO)[:, None] % P).reshape(-1)
def states(rng):
    return (0.125 + 1.375 * rng.random((N, 8, 16, W))) * rng.choice(np.array([0.75, 1.0, 1.25]), (N, 8, 16, 1))
def parts(rng, few=(4, 6, 10, 16, 32)):
    o = rng.permutation(NN).reshape(NN // 32, 32); cl = np.empty(NN, np.int64); cl[o.reshape(-1)] = np.arange(NN) // 32
    sz = rng.permutation(np.resize(np.array(few), NN // 32))[cl]
    def member(c, n, shape, stray):
        m = o[c, (rng.random(shape) * n).astype(np.int64)]
        return np.where(rng.random(shape) < stray, rng.integers(0, NN, shape), m)
    ka = member(cl, sz, (N, 8, 16, NN), 0.04)
    for c in range(5):
        e = member(cl, sz, (N, 8, NN), 0.0); np.put_along_axis(ka, (e & 3)[:, :, None], e[:, :, None], 2)
    nm = 8 * member(cl, 32, (N, 8, 8, NN), 0.2) + rng.integers(0, 8, (N, 8, 8, NN))
    own = np.take_along_axis(ka, rng.integers(0, 4, (N, 8, 1, NN)), 2)[:, :, 0]
    wide_ = np.where(rng.random((N, 8, NN)) < 0.2, 32, sz)
    pv = np.where(rng.random((N, 8, NN)) < 0.35, own, member(cl, wide_, (N, 8, NN), 0.03))
    own = np.take_along_axis(ka[..., ACT], rng.integers(0, 4, (N, 8, 1, RO * LN)), 2)[:, :, 0]
    sp = np.where(rng.random((N, 8, RO * LN)) < 0.6, own, member(cl[ACT], 32, (N, 8, RO * LN), 0.1))
    proto = rng.integers(0, 4, (N, 8, 16, NN // 32))[..., cl]
    xa = np.where(rng.random((N, 8, 16, NN)) < 0.3, proto, rng.integers(0, 4, (N, 8, 16, NN)))
    return ka, nm, xa, pv, sp
def pack(ka, nm, xa, s, pv, sp):
    return {"ka": np.ascontiguousarray(ka).reshape(N, 128, NN).astype(np.int32), "nm": np.ascontiguousarray(nm).reshape(N, 64, NN).astype(np.int32),
            "xa": np.ascontiguousarray(xa).reshape(N, 128, NN).astype(np.float32).astype(BF), "s0": np.ascontiguousarray(s).reshape(N, 128, W).astype(np.float32).astype(BF),
            "pv": np.ascontiguousarray(pv).astype(np.int32), "sp": np.ascontiguousarray(sp).astype(np.int32)}
def setup_inputs(rng):
    ka, nm, xa, pv, sp = parts(rng)
    return pack(ka, nm, xa, states(rng), pv, sp)
def setup_inputs_spread(rng):
    ka, nm, xa, pv, sp = parts(rng)
    s = (0.125 + 0.875 * rng.random((N, 8, 16, W))) * np.exp2(rng.integers(-1, 2, (N, 8, 1, W)))
    s = np.where(rng.random((N, 8, 1, W)) > 0.0625, s, 0.0625)
    return pack(ka, nm, xa, s, pv, sp)
def setup_inputs_ends(rng):
    ka, nm, xa, pv, sp = parts(rng)
    def ends(x, hi, share):
        return np.where(rng.random(x.shape) < share, hi * rng.integers(0, 2, x.shape), x)
    kind = rng.integers(0, 4, (N, 8, 1, NN))
    ka = np.where(kind == 0, 0, np.where(kind == 1, NN - 1, ends(ka, NN - 1, 0.7)))
    nm = ends(nm, W - 1, 0.8); pv = ends(pv, NN - 1, 0.75); sp = ends(sp, NN - 1, 0.75)
    kind = rng.integers(0, 4, (N, 8, 1, NN))
    xa = np.where(kind == 0, 0, np.where(kind == 1, 3, 3 * rng.integers(0, 2, (N, 8, 16, NN))))
    u = P * (LN - 1); v = 0 if u == NN - 1 else NN - 1
    ka[:, :, :15, u] = 0; ka[:, :, 15, u] = NN - 1
    ka[:, :, 1:7, v] = 0; ka[:, :, 8:15, v] = rng.integers(0, NN - 3, (N, 8, 7)); ka[:, :, 15, v] = NN - 1
    ka[:, 0::2, 0, v] = 2; ka[:, 0::2, 7, v] = NN - 3; ka[:, 1::2, 0, v] = NN - 3; ka[:, 1::2, 7, v] = 2
    nm[:, :, 7, v] = W - 1; pv[:, :, u] = v
    for z in (2, NN - 3):
        xa[0::2, :, :, z] = xa[0::2, :, :, u]; xa[1::2, :, :, z] = 3 - xa[1::2, :, :, u]
    u2 = P * (LN - 2); v2 = 1
    ka[:, :, :, u2] = 5; ka[:, :, :7, v2] = 5; ka[:, :, 7, v2] = 0; ka[:, :, 8:, v2] = 5
    pv[:, :, u2] = v2; sp[:, :, LN - 2] = 7; xa[1::2, :, :, 0] = 3 - xa[1::2, :, :, u2]
    s = np.where(rng.random((N, 8, 16, W)) < 0.65, 2.0 - 1.9375 * rng.integers(0, 2, (N, 8, 16, W)), states(rng))
    s[..., W - 2] = 2.0625 - s[..., W - 1]
    return pack(ka, nm, xa, s, pv, sp)
def setup_inputs_corners(rng):
    ka, nm, xa, pv, sp = parts(rng); u = np.arange(NN); h = NN // 2
    for q in range(N):
        for g in range(8):
            c = (g + q) % 8
            if c == 0: pv[q, g] = u; sp[q, g] = ACT
            if c == 1: ka[q, g] = rng.integers(0, NN, NN)[None, :]
            if c == 2:
                ka[q, g] = 2 * rng.integers(0, h, (16, NN)) + (u >= h)[None, :]
                pv[q, g] = np.where(u < h, h + rng.integers(0, h, NN), rng.integers(0, h, NN))
            if c == 3:
                ka[q, g, :15] = rng.integers(0, h, (15, NN)); ka[q, g, 15] = NN - 1; nm[q, g, 7] = 8 * rng.permutation(NN) + 7
            if c == 4: xa[q, g] = 3
            if c == 5:
                ka[q, g, :7] = np.arange(7)[:, None]; ka[q, g, 8:15] = np.arange(7)[:, None]; ka[q, g, 15] = 0; ka[q, g, 7] = rng.integers(7, NN, NN)
            if c == 6: ka[q, g] = rng.permutation(NN)[:16][np.argsort(rng.random((16, NN)), axis=0)]
            if c == 7:
                pv[q, g] = NN - 1 if rng.random() < 0.5 else int(rng.integers(0, NN)); sp[q, g] = int(rng.integers(1, NN))
                k = rng.integers(0, 3, NN)[None, :]
                off = np.where(k == 0, 0, np.where(k == 1, (np.arange(16) == 15)[:, None].astype(np.int64), 1))
                xa[q, g] = (rng.integers(0, 4, (16, 1)) + off) & 3
    return pack(ka, nm, xa, states(rng), pv, sp)
def setup_inputs_ties(rng):
    ka, nm, xa, pv, sp = parts(rng, (4, 8, 16, 32))
    row = rng.integers(0, 16, (N, 8, 1, 1)); flip = rng.integers(0, 2, (N, 8, 1, NN))
    xa = (rng.integers(0, 4, (N, 8, 16, 1)) + (np.arange(16)[:, None] == row) * flip) & 3
    ka[:, :, 8:, ::2] = ka[:, :, :8, ::2]; ka[:, :, 5:8, 1::2] = ka[:, :, 3:4, 1::2]
    return pack(ka, nm, xa, states(rng), pv, sp)
def check_ranges(d):
    bad = []
    for k, lo, hi in (("ka", 0, NN - 1), ("nm", 0, W - 1), ("xa", 0, 3), ("pv", 0, NN - 1), ("sp", 0, NN - 1)):
        v = np.asarray(d[k]).astype(np.float64)
        if not (np.min(v) >= lo and np.max(v) <= hi and np.all(v == np.floor(v))): bad.append("range of " + k)
    v = np.asarray(d["s0"]).astype(np.float64)
    if not (np.min(v) >= 0.0625 and np.max(v) <= 2): bad.append("range of s0")
    return bad
def reference(ka, nm, xa, s0, pv, sp):
    a = ka.astype(np.int64).reshape(N, 8, 16, NN); x = xa.astype(np.float32).reshape(N, 8, 16, NN); S = s0.astype(np.float64).reshape(N, 8, 16, W)
    own = np.broadcast_to(8 * np.arange(NN)[None, :] + np.arange(8)[:, None], (N, 8, 8, NN))
    nam = np.concatenate([own, nm.astype(np.int64).reshape(N, 8, 8, NN)], axis=2)
    p = pv.astype(np.int64).reshape(N, 8, NN); spare = sp.astype(np.int64).reshape(N, 8, RO * LN); out = np.zeros((N, 8, 16, RO * LN))
    for t in range(RO):
        u = P * np.arange(LN) + t % P; v = p[:, :, u]
        au = a[:, :, :, u]; su = nam[:, :, :, u]
        av = np.take_along_axis(a, v[:, :, None], 3); nv = np.take_along_axis(nam, v[:, :, None], 3)
        eq = au[:, :, :, None, :] == av[:, :, None, :, :]
        m = np.where(np.any(eq, axis=3), np.take_along_axis(nv, np.argmax(eq, axis=3), 2), su)
        left = np.take_along_axis(S, su.reshape(N, 8, 1, 16 * LN), 3); right = np.take_along_axis(S, m.reshape(N, 8, 1, 16 * LN), 3)
        gate = 0.5 + 0.5 * np.tanh(0.5 * left)
        O = np.sum((gate * right).reshape(N, 8, 16, 16, LN), axis=3)
        out[:, :, :, t * LN:(t + 1) * LN] = O
        c = av[:, :, :8]; ok = (c != u) & ~np.any(eq, axis=2)[:, :, :8]
        xw = np.take_along_axis(x, c.reshape(N, 8, 1, 8 * LN), 3).reshape(N, 8, 16, 8, LN)
        cnt = np.sum(xw == x[:, :, :, u][:, :, :, None, :], axis=2)
        j = np.argmax(np.where(ok, cnt, -1), axis=2); some = np.any(ok, axis=2)
        w = np.where(some, np.take_along_axis(c, j[:, :, None], 2)[:, :, 0], spare[:, :, t * LN:(t + 1) * LN])
        p[:, :, u] = w
        if t == RO - 1: break
        row = v & 3; place = 8 * u + row
        same = np.take_along_axis(au, row[:, :, None], 2) == v[:, :, None]
        new = np.tanh(0.125 * O + np.where(same, np.take_along_axis(S, place[:, :, None], 3), 0.0))
        sh = 1 + t % (N - 1)
        gv = np.roll(np.roll(v, sh, axis=0), 1, axis=1); gnew = np.roll(np.roll(new, sh, axis=0), 1, axis=1); grow = 4 + (gv & 3)
        np.put_along_axis(S, place[:, :, None], new, 3); np.put_along_axis(S, (8 * u + grow)[:, :, None], gnew, 3)
        rr = 8 + (w & 7); an = np.array(au); nn = np.array(su)
        np.put_along_axis(an, row[:, :, None], v[:, :, None], 2); np.put_along_axis(an, grow[:, :, None], gv[:, :, None], 2)
        np.put_along_axis(an, rr[:, :, None], np.where(some[:, :, None], w[:, :, None], np.take_along_axis(au, rr[:, :, None], 2)), 2)
        np.put_along_axis(nn, rr[:, :, None], np.where(some[:, :, None], (8 * v + j)[:, :, None], np.take_along_axis(su, rr[:, :, None], 2)), 2)
        a[:, :, :, u] = an; nam[:, :, :, u] = nn
    return {"yo": out.reshape(N, 128, RO * LN).astype(np.float32), "yp": p.astype(np.float32)}

def check_inputs(d):
    bad = list(check_ranges(d))
    if not bad:
        for name, y in reference(**d).items():
            for q in range(N):
                v = np.abs(np.asarray(y[q], np.float64)); s = np.sqrt(np.mean(v * v))
                if v.max() > 4 * s or s < 2.0 ** 1: bad.append('%s of rank %d is uneven or too small' % (name, q))
    return bad

import math
from concourse.bass import DstId, RemoteDMATransfer
from concourse.mybir import dt, AluOpType, AxisListType, ActivationFunctionType

N, NN, LN, RO, W = 4, 512, 256, 6, 4096
VW = 288
NPE = 128
CHUNKS = [(128, 16), (0, 64), (64, 64), (144, 64), (208, 48)]
E_ON_ACT = True
SAME_WAR_WAIT = True
BIG = 131072.0
LNB = math.log(1.75)

MATS = (["B%d" % j for j in range(16)] + ["N%d" % j for j in range(8, 16)] +
        ["I", "NI", "E8", "E8lo", "E8hi", "SN", "I256", "PERM", "TH", "BH0", "BH1", "NBH0", "NBH1", "YF0", "YF1", "YS0", "YS1",
         "DF0", "DF1", "DJ0", "DJ1", "A1y", "A1d", "A2y", "A2d", "IHI", "CYh", "CYl", "MN", "Sb0", "Sb1", "Sa0", "Sa1", "REP", "BLK", "M4I", "M4P"])
COLS = ["r", "gp", "p8", "r7", "r3", "p", "lo8", "hi8", "lo4", "mid4", "lo8e", "hi8e", "lo8s", "hi8s", "lo8n", "hi8n", "lo8j", "hi8j",
        "lo4q", "mid4q", "gp2", "gp21", "r15", "w4", "lo88", "hi88", "cs", "cs2", "tb", "cyh", "cyl", "h256", "r16", "t0", "t1"]

SCRATCH = {
    "MT": ("sbuf", [128, 128 * len(MATS)], "bfloat16"),
    "WL": ("sbuf", [128, 144], "bfloat16"), "WS": ("sbuf", [128, 144], "bfloat16"), "W4": ("sbuf", [128, 144], "float16"),
    "I16": ("sbuf", [128, 128], "float16"), "I32": ("sbuf", [128, 128], "float32"), "P32": ("sbuf", [128, 128], "float32"),
    "IP": ("sbuf", [128, 8], "int32"), "CI": ("sbuf", [128, 8], "int32"), "CF": ("sbuf", [128, 40], "float32"),
    "OH": ("sbuf", [128, 16], "float32"), "NCO": ("sbuf", [128, 16], "float32"),
    "T1": ("sbuf", [128, 144], "bfloat16"), "ONE": ("sbuf", [128, 512], "bfloat16"), "GM": ("sbuf", [128, 128], "bfloat16"),
    "H8": ("sbuf", [128, 128], "bfloat16"),
    "UC": ("sbuf", [128, 512], "bfloat16"), "USH": ("sbuf", [128, 256], "bfloat16"),
    "CC0": ("sbuf", [128, 48], "bfloat16"), "CC": ("sbuf", [128, 48], "bfloat16"), "CT": ("sbuf", [128, 96], "bfloat16"),
    "C256": ("sbuf", [128, 256], "bfloat16"),
    "D0L": ("sbuf", [128, 1024], "bfloat16"), "D0H": ("sbuf", [128, 1152], "bfloat16"), "D0F": ("sbuf", [128, 1024], "bfloat16"),
    "KI": ("sbuf", [128, 512], "int32"), "NI_": ("sbuf", [128, 256], "int32"), "NA": ("sbuf", [128, 256], "int32"),
    "NB": ("sbuf", [128, 256], "int32"), "NAb": ("sbuf", [128, 256], "bfloat16"), "NBb": ("sbuf", [128, 256], "bfloat16"),
    "PVI": ("sbuf", [128, 512], "int32"), "PVb": ("sbuf", [128, 512], "bfloat16"),
    "SPI": ("sbuf", [128, 256], "int32"), "SPb": ("sbuf", [128, 256], "bfloat16"),
    "X": ("sbuf", [128, 512], "bfloat16"), "XU": ("sbuf", [128, 4096], "bfloat16"),
    "TB": ("sbuf", [128, 1024], "bfloat16"), "SB": ("sbuf", [128, W + 16], "float32"),
    "VM": ("sbuf", [128, 6 * VW], "bfloat16"), "VL": ("sbuf", [128, 5 * VW], "bfloat16"),
    "TS": ("sbuf", [128, 5 * 256], "float32"), "TL": ("sbuf", [128, 5 * 256], "float32"),
    "VWU": ("sbuf", [128, 96], "uint16"),
    "AVK": ("sbuf", [128, 256], "bfloat16"), "AVN": ("sbuf", [128, 256], "bfloat16"),
    "ZL": ("sbuf", [128, 2048], "bfloat16"), "LS": ("sbuf", [128, 2048], "bfloat16"), "EE": ("sbuf", [128, 2048], "bfloat16"),
    "ZH": ("sbuf", [128, 2304], "float32"), "HS": ("sbuf", [128, 2304], "float32"),
    "QI": ("sbuf", [128, 256], "int32"), "QM": ("sbuf", [128, 256], "int32"),
    "SU": ("sbuf", [128, 6 * 256], "uint16"), "MU": ("sbuf", [128, 6 * 256], "uint16"), "LU": ("sbuf", [128, 5 * 48], "uint16"),
    "KU": ("sbuf", [128, 128], "uint16"), "SF": ("sbuf", [128, 128], "bfloat16"), "NE": ("sbuf", [128, 2048], "bfloat16"),
    "TM": ("sbuf", [128, 128], "bfloat16"), "F": ("sbuf", [128, 128], "bfloat16"), "FK": ("sbuf", [128, 128], "bfloat16"),
    "XS": ("sbuf", [128, 256], "bfloat16"), "RB": ("sbuf", [128, 256], "bfloat16"), "M": ("sbuf", [128, 256], "bfloat16"),
    "DN": ("sbuf", [128, 256], "float32"), "DMK": ("sbuf", [128, 256], "float16"), "DMN": ("sbuf", [128, 256], "float16"),
    "GT": ("sbuf", [128, 4096], "float32"), "PR": ("sbuf", [128, 4096], "float32"), "SCN": ("sbuf", [128, 4096], "float32"),
    "OB": ("sbuf", [128, 6 * 256], "float32"), "HH": ("sbuf", [128, 256], "float32"), "ZZ": ("sbuf", [128, 256], "float32"),
    "UB": ("sbuf", [128, 256], "float32"), "YP": ("sbuf", [128, 512], "float32"),
    "pz0": ("psum", [128, 512], "float32"), "pz1": ("psum", [128, 512], "float32"),
    "pa": ("psum", [128, 512], "float32"), "pb": ("psum", [128, 512], "float32"), "pc": ("psum", [128, 512], "float32"),
    "pd": ("psum", [128, 512], "float32"), "pe": ("psum", [128, 512], "float32"), "pf": ("psum", [128, 512], "float32"),
}
SEMAPHORES = (["cP", "cV", "cA", "cG", "sent", "outs", "lsp", "lpv", "lka", "lnm", "lxa", "ls0"] +
              ["av%d" % t for t in range(5)] + ["at%d" % t for t in range(5)])

ALU = AluOpType
AF = ActivationFunctionType
GATH, SCAT = 1j, -1
MODELS = [(0.0010, 0.0005, 1.55, 3.8, 0.15, 1.0, 1.0), (0.00085, 0.00043, 1.1, 2.0, 0.08, 0.8, 1.0),
          (0.0012, 0.0006, 2.0, 5.5, 0.25, 1.4, 1.5), (0.0010, 0.0008, 1.55, 3.8, 0.15, 1.0, 1.0)]
WEIGHTS = [1.0, 1.0, 1.0, 0.5]
ROUNDS, MOVES, STEP = 3000, 6, 8.0
ORDER = {}


def cost(x, m):
    fixed, n = x["cost"]
    if x["eng"] == "P":
        return fixed + n * m[1]
    if isinstance(n, complex):
        n = n.imag * m[2]
    elif n < 0:
        n = -n * m[3]
    return fixed * m[6] + n * m[0]


def build(g, core, T, topo, rank):
    nodes = []
    lastw, readers, bank = {}, {}, {}

    def add(eng, fn, cost, rd=(), wr=(), bk=(), lat=0.0, sem=None, after=()):
        me = len(nodes)
        deps = {}

        def dep(i, raw):
            same = nodes[i]["eng"] == eng and nodes[i]["sem"] is None and sem is None
            need = (not same) or (eng != "P" and (raw or SAME_WAR_WAIT))
            deps[i] = deps.get(i, False) or need
        for k in rd:
            if k in lastw:
                dep(lastw[k], True)
        for k in wr:
            if k in lastw:
                dep(lastw[k], False)
            for i in readers.get(k, ()):
                dep(i, False)
        for b in bk:
            if b in bank:
                i = bank[b]
                deps[i] = deps.get(i, False) or nodes[i]["eng"] != eng
            bank[b] = me
        for i in after:
            deps[i] = deps.get(i, False)
        for k in rd:
            readers.setdefault(k, []).append(me)
        for k in wr:
            lastw[k] = me
            readers[k] = []
        nodes.append({"eng": eng, "fn": fn, "cost": cost, "lat": lat, "deps": deps, "sem": sem, "tag": (list(wr) + ["-"])[0]})
        return me

    def V(fn, n, rd, wr, bk=()):
        return add("V", fn, (0.05, n if isinstance(n, complex) or n < 0 else max(n, 64)), rd, wr, bk)

    def A(fn, n, rd, wr, bk=()):
        return add("A", fn, (0.08, n if isinstance(n, complex) else max(n, 64)), rd, wr, bk)

    def G(fn, n, wr, rd=()):
        return add("G", fn, (0.15, 2 * n), rd, wr)

    def P(mms, rd, wr, b, f32=False, first=True, last=True):
        def fn():
            for i, (o, l, r, n) in enumerate(mms):
                ins = g.tensor.matmul(o, l, r, first and i == 0, last and i == len(mms) - 1)
            return ins
        return add("P", fn, (0.03, sum(max(64, m[3]) for m in mms) * (4 if f32 else 1)), rd, wr, (b,))

    def mat(n):
        i = MATS.index(n)
        return T.MT[:, 128 * i:128 * i + 128]

    def col(n, k=1):
        i = COLS.index(n)
        return T.CF[:, i:i + k]

    v, a = g.vector, g.scalar

    def ts(out, in0, s1, s2, o0, o1=None):
        if o1 is None:
            return lambda: v.tensor_scalar(out, in0, s1, None, o0)
        return lambda: v.tensor_scalar(out, in0, s1, s2, o0, o1)

    def tt(out, i0, i1, op):
        return lambda: v.tensor_tensor(out, i0, i1, op)

    def cp(out, i):
        return lambda: v.tensor_copy(out, i)

    def ms(out, c):
        return lambda: v.memset(out, c)

    def act(out, i, f, bias=0.0, scale=1.0):
        return lambda: a.activation(out, i, f, bias=bias, scale=scale)

    def dma(eng, out, src, sem, rd, wr, lat, count=16):
        q = {"S": g.sync, "A": a, "G": g}[eng]
        return add(eng, lambda: q.dma_start(out, src).then_inc(T.sem[sem], 16), (1.0 if eng == "G" else 0.1, 0), rd, wr,
                   lat=lat, sem=(sem, count))

    sent = [0]

    def exchange(t, src, dst, sem, rd, wr, lat):
        sh = 1 + t % (N - 1)
        to, frm = T.cores[(rank + sh) % N], T.cores[(rank - sh) % N]
        rid, pid, se = topo.addr(to)
        sent[0] += len(topo.engines(core, to))
        s = add("G", lambda: g.remote_dma(dst, src, T.sem[sem], T.sem.sent, pid, rid, topo.mask(core, to)), (0.6, 0), rd, (),
                sem=("sent", None))
        add(None, None, (0.0, 0), (), wr, lat=lat, sem=(sem, len(topo.engines(frm, core))), after=(s,))

    dma("S", T.PVI[0:8, :], T.pv[:, :], "lpv", (), ["PVI"], 2.0)
    dma("S", T.KI[:, :], T.ka[:, :], "lka", (), ["KI"], 2.2)
    dma("A", T.NI_[:, :], T.nm[:, :], "lnm", (), ["NI_"], 2.2)
    dma("A", T.X[:, :], T.xa[:, :], "lxa", (), ["X"], 2.2)
    G(lambda: g.iota(T.SPI[:, :], [[0, 256]], 0, 0), 256, ["SPI0"])
    last = None
    for t in range(RO):
        last = dma("S", T.SPI[t:128:16, :], T.sp[:, t * LN:(t + 1) * LN], "lsp", ["SPI0"], ["SPI%d" % (t + 1)], 2.0, 96)
    dma("G", T.SB[:, 8:W + 8], T.s0[:, :], "ls0", (), ["S"], 6.0)
    V(ms(T.SB[:, 0:8], 0.0), 8, (), ["Sp0"])
    V(ms(T.SB[:, W + 8:W + 16], 0.0), 8, (), ["Sp1"])

    def iota(out, pat, base, cm, n, key, flag=True):
        if flag:
            G(lambda: g.iota(out, pat, base, cm, allow_small_or_imprecise_dtypes=True), n, [key])
        else:
            G(lambda: g.iota(out, pat, base, cm), n, [key])
    iota(T.IP[:, 0:1], [[0, 1]], 0, 1, 1, "IP", False)
    iota(T.T1[:, :], [[1, 144]], 0, -1, 144, "T1")
    iota(T.GM[:, :], [[1, 8], [0, 16]], 0, 0, 128, "GM")
    iota(T.H8[:, :], [[1, 16], [0, 8]], 0, 0, 128, "H8")
    V(ms(T.ONE[:, :], 1.0), 256, (), ["ONE"])

    def sel(out, keys, pat, base, n, rows=128):
        G(lambda: g.affine_select(out, T.ONE[0:rows, 0:n], pat, ALU.is_equal, 0.0, base, 1), n, keys, ["ONE"])
    ri = MATS.index("REP")
    sel(T.MT[0:8, 128 * ri:128 * ri + 128], ["REP"], [[-1, 8], [0, 16]], 0, 128, 8)
    for j in range(0, 16, 4):
        sel(T.MT[:, 128 * j:128 * j + 512], ["B%d" % i for i in range(j, j + 4)], [[-1, 4], [-16, 8], [0, 16]], -j, 512)
    for h in range(2):
        sel(mat("Sb%d" % h), ["Sb%d" % h], [[-16, 8], [1000, 2], [-2, 8]], -h, 128)
        sel(mat("Sa%d" % h), ["Sa%d" % h], [[-16, 8], [1000, 2], [-2, 8]], -1000 - h, 128)
    sel(mat("MN"), ["MN"], [[-16, 8], [0, 2], [-1, 8]], -8, 128)
    iota(T.UC[:, :], [[1, 512]], -256, 0, 512, "UC")
    iota(T.CC0[:, :], [[0, 3], [1, 16]], 0, 0, 48, "CC0")
    ip = T.IP[:, 0:1]
    for i, (s, op) in enumerate([(15, ALU.bitwise_and), (4, ALU.arith_shift_right), (3, ALU.arith_shift_right), (7, ALU.bitwise_and),
                                 (3, ALU.bitwise_and), (255, ALU.bitwise_and)]):
        V(ts(T.CI[:, i:i + 1], ip, s, None, op), 1, ["IP"], ["CI%d" % i])
    V(cp(T.CF[:, 0:6], T.CI[:, 0:6]), 6, ["CI%d" % i for i in range(6)], ["r", "gp", "p8", "r7", "r3", "p"])

    def C(name, src, s1, s2, o0, o1=None, k=1, rd=()):
        i, j = COLS.index(name), COLS.index(src)
        V(ts(col(name, k), col(src, k), s1, s2, o0, o1), k, list(COLS[j:j + k]) + list(rd), COLS[i:i + k])
    C("lo8", "r", 8.0, None, ALU.is_lt)
    C("hi8", "r", 8.0, None, ALU.is_ge)
    C("lo4", "r", 4.0, None, ALU.is_lt)
    C("mid4", "lo8", col("lo4"), None, ALU.subtract, rd=["lo4"])

    def CA(name, src, scale, bias, k=1):
        i, j = COLS.index(name), COLS.index(src)
        A(act(col(name, k), col(src, k), AF.Identity, col(bias) if isinstance(bias, str) else bias, col(scale) if isinstance(scale, str) else scale),
          k, list(COLS[j:j + k]) + [s for s in (scale, bias) if isinstance(s, str)], COLS[i:i + k])
    CA("lo8j", "lo8", "r7", 0.0, 2)
    CA("lo4q", "lo4", 0.25, 0.0, 2)
    CA("gp2", "gp", 2.0, 0.0)
    CA("gp21", "gp", 2.0, 1.0)
    C("r15", "r", -1.0, 15.0, ALU.mult, ALU.add)
    CA("w4", "lo4", 8192.0, 0.0)
    C("lo88", "lo8", 8.0, None, ALU.mult, k=2)
    CA("cs", "lo8j", 1.0, 2048.0)
    CA("cs2", "lo8j", 1.0, 38912.0)
    CA("tb", "r7", -LNB, -8.0)
    CA("cyh", "lo8", 32.0 / 256, 161.0 / 256)
    C("t0", "r3", -0.25 / 256, col("lo8"), ALU.mult, ALU.mult, rd=["lo8"])
    CA("t1", "r7", -0.125 / 256, 0.0625 / 256)
    CA("cyl", "t1", "hi8", "t0")
    CA("h256", "hi8", 256.0, 0.0)
    CA("r16", "r", 0.0625, 0.0)

    def Mx(out, key, src, skey, s1, s2=None, n=64):
        rd = [skey] + [s for s in (s1, s2) if isinstance(s, str)]
        x1 = col(s1) if isinstance(s1, str) else float(s1)
        if s2 is None:
            V(ts(out, src, x1, None, ALU.is_equal), n, rd, [key])
        else:
            V(ts(out, src, x1, col(s2) if isinstance(s2, str) else float(s2), ALU.is_equal, ALU.mult), n, rd, [key])
    t1 = T.T1[:, 0:128]

    def Ms(out, key, base, s, rd=()):
        A(act(out, mat(base), AF.Identity, 0.0, col(s) if isinstance(s, str) else float(s)), 128,
          [base] + list(rd) + ([s] if isinstance(s, str) else []), [key])
    Mx(T.WL[:, :], "WL", T.T1[:, :], "T1", "r15", 8.0)
    Mx(T.W4[:, :], "W4", T.T1[:, :], "T1", "r15", "w4")
    Mx(T.WS[:, :], "WS", T.T1[:, :], "T1", 8, "lo8")
    for n, s in (("I", None), ("NI", -1.0), ("E8hi", "hi88")):
        Mx(mat(n), n, t1, "T1", 0, s)
    for n, s in (("E8", 8.0), ("E8lo", "lo88"), ("I256", 256.0), ("A1y", "lo4q"), ("A1d", "lo4"), ("IHI", "hi8"), ("CYh", "cyh"), ("CYl", "cyl")):
        Ms(mat(n), n, "I", s)
    Mx(T.I16[:, :], "I16", t1, "T1", 0)
    Ms(T.I32[:, :], "I32", "I", 1.0)
    i = 128 * MATS.index("PERM")
    Mx(T.MT[:, i + 16:i + 128], "PERMx", T.T1[:, 16:128], "T1", 16)
    Mx(T.MT[:, i:i + 16], "PERM", T.T1[:, 0:16], "T1", -112)
    Ms(mat("A2y"), "A2y", "PERM", "mid4q", ["PERMx"])
    Ms(mat("A2d"), "A2d", "PERM", "mid4", ["PERMx"])
    Ms(T.P32[:, :], "P32", "PERM", 1.0, ["PERMx"])
    V(tt(mat("SN"), mat("E8hi"), T.WS[:, 0:128], ALU.add), 256, ["E8hi", "WS"], ["SN"])
    Mx(mat("TH"), "TH", T.H8[:, :], "H8", "p8", 0.3984375)
    for h, s in ((0, "lo8"), (1, "hi8")):
        Mx(mat("BH%d" % h), "BH%d" % h, T.GM[:, :], "GM", "gp", s)
        Ms(mat("NBH%d" % h), "NBH%d" % h, "BH%d" % h, -1.0)
        Mx(mat("DF%d" % h), "DF%d" % h, T.H8[:, :], "H8", "gp21", s)
        Ms(mat("YF%d" % h), "YF%d" % h, "DF%d" % h, 0.125)
        Ms(mat("YS%d" % h), "YS%d" % h, "DF%d" % h, -0.0625)
        Mx(mat("DJ%d" % h), "DJ%d" % h, T.H8[:, :], "H8", "gp2", s + "j")
    Mx(T.OH[:, :], "OH", T.CC0[:, 0:16], "CC0", "r", 1.0 / BIG)
    V(ts(T.NCO[:, 8:16], T.OH[:, 8:16], 8.0, None, ALU.mult), 8, ["OH"], ["NC1"])
    V(tt(T.NCO[:, 0:8], T.NCO[:, 8:16], T.OH[:, 0:8], ALU.add), 8, ["OH", "NC1"], ["NC"])
    Mx(mat("BLK"), "BLK", T.GM[:, :], "GM", "gp")
    for j in range(8, 16):
        A(act(mat("N%d" % j), mat("BLK"), AF.Identity, 0.0, T.NCO[:, j - 8:j - 7]), 128, ["BLK", "NC"], ["N%d" % j])
    Ms(mat("M4I"), "M4I", "I", -4.0)
    Ms(mat("M4P"), "M4P", "PERM", -4.0, ["PERMx"])
    V(ts(T.USH[:, :], T.UC[:, 0:256], col("h256"), None, ALU.add), 128, ["UC", "h256"], ["USH"])
    A(act(T.CC[:, :], T.CC0[:, :], AF.Identity, col("r16")), 48, ["CC0", "r16"], ["CC"])
    for par in range(2):
        iota(T.CT[:, 48 * par:48 * par + 16], [[0, 16]], 784 + 8 * par, 0, 16, "CTa%d" % par)
        iota(T.CT[:, 48 * par + 16:48 * par + 48], [[0, 32]], 780 + 8 * par, 0, 32, "CT%d" % par)
    iota(T.C256[:, :], [[0, 256]], 256, 0, 256, "C256")
    V(ms(T.D0L[:, :], -1.0), 512, (), ["D0La"])
    V(ms(T.D0L[:, 0:1024:8], 2.0 ** 30), 64, ["D0La"], ["D0L"])
    iota(T.D0H[:, :], [[0, 1152]], -4096, 0, 1152, "D0Ha")
    V(ms(T.D0H[:, 0:1152:9], 2.0 ** 30), 64, ["D0Ha"], ["D0H"])
    if NPE < LN:
        for h in range(2):
            G((lambda h: lambda: g.affine_select(T.D0F[:, 512 * h:512 * h + 512], T.ONE[:, :], [[0, 32], [1, 16]], ALU.not_equal, 0.0, 0, 0))(h),
              512, ["D0F%d" % h], ["ONE"])

    V(ts(T.PVb[0:8, :], T.PVI[0:8, :], -256.0, None, ALU.add), 512, ["PVI"], ["PVb"])
    V(ts(T.TB[:, 0:512], T.KI[:, :], -256.0, None, ALU.add), 512, ["KI"], ["K"])
    V(ts(T.NA[:, :], T.NI_[:, :], 3, None, ALU.arith_shift_right), 256, ["NI_"], ["NA"])
    V(ts(T.NB[:, :], T.NI_[:, :], 7, None, ALU.bitwise_and), 256, ["NI_"], ["NB"])
    V(ts(T.NAb[:, :], T.NA[:, :], -256.0, None, ALU.add), 256, ["NA"], ["NAb"])
    V(cp(T.NBb[:, :], T.NB[:, :]), 256, ["NB"], ["NBb"])
    for h in range(2):
        o = T.pd[:, 256 * h:256 * h + 256]
        P([(o, mat("Sb%d" % h), T.NBb[:, :], 256), (o, mat("Sa%d" % h), T.NAb[:, :], 256)], ["Sb%d" % h, "Sa%d" % h, "NAb", "NBb"], ["pd%d" % h], "pd")
    A(act(T.TB[:, 512:1024], T.pd[:, :], AF.Identity), 512, ["pd0", "pd1"], ["TN"], ["pd"])
    V(ts(T.SPb[:, :], T.SPI[:, :], -256.0, None, ALU.add), 256, ["SPI%d" % i for i in range(7)], ["SPb"])
    for par in range(2):
        for s in range(16):
            h = s // 8
            o, i = T.XU[:, 2048 * par + s:2048 * (par + 1):16], T.X[:, 256 * h + par:256 * h + 256:2]
            if s % 4 == 3 or par:
                A(act(o, i, AF.Identity), 128, ["X"], ["XU%d_%d" % (par, s)])
            else:
                V(cp(o, i), 64, ["X"], ["XU%d_%d" % (par, s)])

    def Vrow(t):
        return T.VM[:, VW * t:VW * t + 256]

    def L(s):
        return T.WL[:, 15 - s:143 - s]

    def partners(t):
        o = T.pe[:, 256:272]
        P([(o, L(s), T.VM[:, VW * t + s:VW * t + 256:16], 16) for s in range(16)], ["WL", "V%d" % t], ["pew"], "pe")
        V(ts(T.VWU[:, 16 * t:16 * t + 16], o, 1.0 / 128, 256.0, ALU.mult, ALU.add), 16, ["pew"], ["VWU%d" % t], ["pe"])
        if t < RO - 1:
            A(act(T.VM[:, VW * t + 256:VW * t + 272], o, AF.Identity, 0.0, 1.0 / 128), 16, ["pew"], ["V3a%d" % t], ["pe"])
            A(act(T.VM[:, VW * t + 272:VW * t + VW], o, AF.Identity, 192.625, 1.0 / 512), 16, ["pew"], ["V3b%d" % t], ["pe"])
            exchange(t, T.VM[:, VW * t:VW * t + VW], T.VL[:, VW * t:VW * t + VW], "av%d" % t, ["V%d" % t, "V3a%d" % t, "V3b%d" % t],
                     ["VL%d" % t], 3.0)

    for t in range(2):
        P([(T.pe[:, 0:256], T.MT[0:8, 128 * ri:128 * ri + 128], T.PVb[0:8, t:512:2], 256)], ["REP", "PVb"], ["peW"], "pe")
        A(act(Vrow(t), T.pe[:, 0:256], AF.Identity), 256, ["peW"], ["V%d" % t], ["pe"])
        partners(t)

    def index_step(t):
        par = t % 2
        AU, TNa = T.TB[:, par:512:2], T.TB[:, 512 + par:1024:2]
        vw, Vt, vk = T.VWU[:, 16 * t:16 * t + 16], Vrow(t), "V%d" % t
        A(act(T.AVK[:, :], T.TB[:, 0:512].indirect(vw), AF.Identity), 256 * GATH, ["K", "VWU%d" % t], ["AVK"])
        A(act(T.AVN[:, :], T.TB[:, 512:1024].indirect(vw), AF.Identity), 256 * GATH, ["TN", "VWU%d" % t], ["AVN"])
        KS = T.pb[:, 0:128]
        P([(KS, T.WS[:, 8 - 8 * h:136 - 8 * h], T.AVK[:, 128 * h:128 * h + 128], 128) for h in range(2)], ["WS", "AVK"], ["KS"], "pb")
        V(ts(T.KU[:, :], KS, 256.0, None, ALU.add), 128, ["KS"], ["KU"], ["pb"])
        V(tt(T.SF[:, :], KS, T.USH[:, par:256:2], ALU.is_equal), 128, ["KS", "USH"], ["SF"], ["pb"])
        for c in range(2):
            V(tt(T.NE[:, 1024 * c:1024 * c + 1024], T.X[:, :].indirect(T.KU[:, 64 * c:64 * c + 64]),
                 T.XU[:, 2048 * par + 1024 * c:2048 * par + 1024 * c + 1024], ALU.not_equal), 1024 * GATH,
              ["X", "KU"] + ["XU%d_%d" % (par, s) for s in range(16)], ["NE%d" % c])
        for j0 in range(0, 16, 2):
            bn = "pz%d" % (j0 // 2 % 2)
            pz = T[bn]
            for j in (j0, j0 + 1):
                o = pz[:, 256 * (j - j0):256 * (j - j0) + 256]
                mm = [(o, mat("B%d" % j), T.AVK[:, :], 256), (o, mat("NI"), AU, 256)]
                rd = ["B%d" % j, "NI", "AVK", "K"]
                if j >= 8:
                    mm.append((o, mat("N%d" % j), T.AVN[:, :], 256))
                    rd += ["N%d" % j, "AVN"]
                P(mm, rd, [bn + "_%d" % (j - j0)], bn)
            for j in (j0, j0 + 1):
                o = pz[:, 256 * (j - j0):256 * (j - j0) + 256]
                if j < 8:
                    A(act(T.ZL[:, j:2048:8], o, AF.Abs, 7.0, BIG), 256, [bn + "_%d" % (j - j0)], ["ZL%d" % j], [bn])
                else:
                    A(act(T.ZH[:, j - 8:2304:9], o, AF.Abs, 38912.0, BIG), 256, [bn + "_%d" % (j - j0)], ["ZH%d" % j], [bn])
        zl = ["ZL%d" % j for j in range(8)]
        for h in range(2):
            sl = slice(1024 * h, 1024 * h + 1024)
            if E_ON_ACT:
                A(act(T.EE[:, sl], T.ZL[:, sl], AF.Relu, 32.0, -1.0 / 1024), 1024, zl, ["EE%d" % h])
            else:
                V(ts(T.EE[:, sl], T.ZL[:, sl], 100.0, 32.0, ALU.is_lt, ALU.mult), 512, zl, ["EE%d" % h])
            V((lambda sl: lambda: v.tensor_tensor_scan(T.LS[:, sl], T.D0L[:, :], T.ZL[:, sl], 0.0, ALU.add, ALU.min))(sl),
              512, zl + ["D0L", "D0La"], ["LS%d" % h])
        so = T.pa[:, 0:256]
        P([(so, mat("SN"), TNa, 256), (so, mat("E8lo"), T.UC[:, par:512:2], 256)], ["SN", "E8lo", "UC", "TN"], ["pas"], "pa")
        V(ts(T.SU[:, 256 * t:256 * t + 256], so, col("cs"), None, ALU.add), 256, ["pas", "cs"], ["SU%d" % t], ["pa"])
        A(act(T.ZH[:, 8:2304:9], so, AF.Identity, col("cs2")), 256, ["pas", "cs2"], ["ZHs"], ["pa"])
        po = T.pa[:, 256:512]
        P([(po, mat("E8"), Vt, 256), (po, mat("E8"), T.C256[:, :], 256), (po, mat("I"), T.LS[:, 7:2048:8], 256)],
          ["E8", "I", "C256", vk, "LS0", "LS1"], ["pap"], "pa")
        zh = ["ZH%d" % j for j in range(8, 16)] + ["ZHs"]
        for h in range(2):
            sl = slice(1152 * h, 1152 * h + 1152)
            V((lambda sl: lambda: v.tensor_tensor_scan(T.HS[:, sl], T.D0H[:, :], T.ZH[:, sl], 0.0, ALU.add, ALU.min))(sl),
              1152, zh + ["D0H", "D0Ha"], ["HS%d" % h])
        V(tt(T.QI[:, :], po, T.HS[:, 8:2304:9], ALU.min), 256, ["pap", "HS0", "HS1"], ["QI"], ["pa"])
        V(ts(T.QM[:, :], T.QI[:, :], W - 1, None, ALU.bitwise_and), 256, ["QI"], ["QM"])
        V(cp(T.MU[:, 256 * t:256 * t + 256], T.QM[:, :]), 256, ["QM"], ["MU%d" % t])
        SC, TO = T.pb[:, 128:256], T.pb[:, 256:384]
        P([(SC, mat("I256"), T.SF[:, :], 128)], ["I256", "SF"], ["SC"], "pb", last=False)
        for q in range(2):
            P([(SC, L(s), T.NE[:, s:2048:16], 128) for s in range(8 * q, 8 * q + 8)], ["WL", "NE0", "NE1"], ["SC"], "pb", first=False, last=False)
        for h in range(2):
            P([(SC, L(8 * h + j), T.EE[:, 1024 * h + j:1024 * h + 1024:8], 128) for j in range(8)], ["WL", "EE%d" % h], ["SC"], "pb",
              first=False, last=h == 1)
        A(act(T.TM[:, :], SC, AF.Sigmoid, col("tb"), -LNB), 128, ["SC", "tb"], ["TM"], ["pb"])
        P([(TO, mat("TH"), T.TM[:, :], 128)], ["TH", "TM"], ["TO"], "pb")
        V(tt(T.F[:, :], TO, T.TM[:, :], ALU.is_lt), 128, ["TO", "TM"], ["F"], ["pb"])
        V(tt(T.FK[:, :], KS, T.F[:, :], ALU.mult), 128, ["KS", "F"], ["FK"], ["pb"])

        def halves(b, c0, name, rhs):
            return [(b[:, c0 + 128 * h:c0 + 128 * h + 128], mat(name + str(h)), rhs, 128) for h in range(2)]
        if t < RO - 1:
            GV = T.VL[:, VW * t:VW * t + 256]
            y, dk, dn = T.pc[:, 0:256], T.pd[:, 0:256], T.pd[:, 256:512]
            P([(y, mat("CYh"), T.C256[:, :], 256), (y, mat("CYl"), T.C256[:, :], 256), (y, mat("A1y"), Vt, 256), (y, mat("A2y"), GV, 256)],
              ["CYh", "CYl", "C256", "A1y", "A2y", vk, "VL%d" % t], ["pc0"], "pc", last=False)
            P(halves(T.pc, 0, "YS", T.F[:, :]) + halves(T.pc, 0, "YF", T.FK[:, :]), ["YS0", "YS1", "YF0", "YF1", "F", "FK"], ["pc0"], "pc", first=False)
            P([(dk, mat("NI"), AU, 256), (dk, mat("A1d"), Vt, 256), (dk, mat("A2d"), GV, 256)],
              ["NI", "K", "A1d", "A2d", vk, "VL%d" % t], ["pd0"], "pd", last=False)
            P(halves(T.pd, 0, "DF", T.FK[:, :]), ["DF0", "DF1", "FK"], ["pd0"], "pd", first=False)
            P([(dn, mat("NI"), TNa, 256), (dn, mat("IHI"), Vt, 256)] + halves(T.pd, 256, "DJ", T.F[:, :]),
              ["NI", "TN", "IHI", vk, "DJ0", "DJ1", "F"], ["pd1"], "pd")
            A(act(T.RB[:, :], y, AF.Identity), 256, ["pc0"], ["RB"], ["pc"])
            A(act(T.DN[:, :], dn, AF.Identity), 256, ["pd1"], ["DN"], ["pd"])
            V(tt(T.M[:, :], y, T.RB[:, :], ALU.is_equal), 256, ["pc0", "RB"], ["M"], ["pc"])
            V(tt(T.DMK[:, :], dk, T.M[:, :], ALU.mult), 256, ["pd0", "M"], ["DMK"], ["pd"])
            mn = T.pc[:, 256:512]
            P([(mn, mat("MN"), T.M[:, :], 256)], ["MN", "M"], ["pc1"], "pc")
            P([(dk, mat("I"), AU, 256), (dk, T.I16[:, :], T.DMK[:, :], 256)], ["I", "I16", "K", "DMK"], ["pd0"], "pd")
            A(act(AU, dk, AF.Identity), 256, ["pd0"], ["K"], ["pd"])
            V(tt(T.DMN[:, :], mn, T.DN[:, :], ALU.mult), 256, ["pc1", "DN"], ["DMN"], ["pc"])
            P([(y, mat("I"), TNa, 256), (y, T.I16[:, :], T.DMN[:, :], 256)], ["I", "I16", "TN", "DMN"], ["pc0"], "pc")
            A(act(TNa, y, AF.Identity), 256, ["pc0"], ["TN"], ["pc"])
            o = T.pe[:, 272:320]
            va, vb = slice(VW * t + 256, VW * t + 272), slice(VW * t + 272, VW * t + VW)
            P([(o, mat("I256"), T.CC[:, :], 48), (o, mat("I"), T.CT[:, 48 * par:48 * par + 48], 48),
               (T.pe[:, 272:288], mat("PERM"), T.VL[:, va], 16), (T.pe[:, 272:288], mat("M4P"), T.VL[:, vb], 16),
               (T.pe[:, 288:304], mat("I"), T.VM[:, va], 16), (T.pe[:, 288:304], mat("M4I"), T.VM[:, vb], 16),
               (T.pe[:, 304:320], mat("I"), T.VM[:, va], 16), (T.pe[:, 304:320], mat("M4I"), T.VM[:, vb], 16)] +
              [(T.pe[:, 304:320], T.W4[:, 15 - s:143 - s], T.DMK[:, s:256:16], 16) for s in range(16)],
              ["I256", "I", "CC", "CT%d" % par, "CTa%d" % par, "PERM", "PERMx", "M4I", "M4P", "VL%d" % t, "V3a%d" % t, "V3b%d" % t, "W4", "DMK"],
              ["pel"], "pe")
            V(ts(T.LU[:, 48 * t:48 * t + 48], o, 0.0, float(W + 8), ALU.max, ALU.min), 48, ["pel"], ["LU%d" % t], ["pe"])
        ns = T.pa[:, 0:256]
        P(halves(T.pa, 0, "NBH", T.F[:, :])[0:1], ["NBH0", "F"], ["pas"], "pa")
        P(halves(T.pa, 0, "NBH", T.F[:, :])[1:2], ["NBH1", "F"], ["pas2"], "pa")
        V(tt(T.XS[:, :], ns, T.SPb[:, :], ALU.mult), 256, ["pas", "pas2", "SPb"], ["XS"], ["pa"])
        wo = T.pe[:, 0:256]
        P([(wo, mat("B%d" % t), T.SPb[:, :], 256), (wo, mat("B%d" % t), T.XS[:, :], 256)] + halves(T.pe, 0, "BH", T.FK[:, :]),
          ["B%d" % t, "SPb", "XS", "BH0", "BH1", "FK"], ["peW"], "pe")
        if t + 2 < RO:
            A(act(Vrow(t + 2), wo, AF.Identity), 256, ["peW"], ["V%d" % (t + 2)], ["pe"])
            partners(t + 2)
        else:
            A(act(T.YP[:, par:512:2], wo, AF.Identity, 256.0), 256, ["peW"], ["YP%d" % par], ["pe"])

    def state_step(t):
        Sw, Sall = T.SB[:, 8:W + 8], T.SB[:, :]
        npe = NPE
        pk, sk = [], []
        for c, (l0, cl) in enumerate(CHUNKS):
            lo, ce, e = 256 * t + l0, 16 * cl, slice(16 * l0, 16 * (l0 + cl))
            A(act(T.GT[:, e], Sw.indirect(T.SU[:, lo:lo + cl]), AF.Sigmoid), ce * GATH, ["S", "SU%d" % t], ["GT%d" % c])
            V(tt(T.PR[:, e], Sw.indirect(T.MU[:, lo:lo + cl]), T.GT[:, e], ALU.mult), ce * GATH, ["S", "MU%d" % t, "GT%d" % c], ["PR%d" % c])
            if l0 < npe:
                o = T.pf[:, l0:l0 + cl]
                pk.append("pf%d" % c)
                for q in range(0, 16, 4):
                    P([(o, T.I32[:, :], T.PR[:, 16 * l0 + k:16 * (l0 + cl):16], cl) for k in range(q, q + 4)], ["I32", "PR%d" % c], ["pf%d" % c],
                      "pf", True, q == 0, q == 12)
            else:
                sk.append("SCN%d" % c)
                V((lambda e, ce: lambda: v.tensor_tensor_scan(T.SCN[:, e], T.D0F[:, 0:ce], T.PR[:, e], 0.0, ALU.mult, ALU.add))(e, ce),
                  ce, ["PR%d" % c, "D0F0", "D0F1"], ["SCN%d" % c])
        PECH, NCH = len(pk), len(CHUNKS)
        so = T.SCN[:, 16 * npe + 15:4096:16]
        if PECH:
            A(act(T.OB[:, 256 * t:256 * t + npe], T.pf[:, 0:npe], AF.Identity), npe, pk, ["OBa%d" % t], ["pf"])
        if t < RO - 1:
            lu = "LU%d" % t
            A(act(T.HH[:, :], Sall.indirect(T.LU[:, 48 * t + 32:48 * t + 48]), AF.Identity, 0.0, 8.0), 256 * GATH, ["S", "Sp0", "Sp1", lu], ["HH"])
            if PECH:
                V(tt(T.ZZ[:, 0:npe], T.pf[:, 0:npe], T.HH[:, 0:npe], ALU.add), npe, pk + ["HH"], ["ZZa"], ["pf"])
            if PECH < NCH:
                V(tt(T.ZZ[:, npe:256], so, T.HH[:, npe:256], ALU.add), 2 * (256 - npe), sk + ["HH"], ["ZZb"])
            zs = T.pf[:, 256:512]
            P([(zs, T.P32[:, :], T.ZZ[:, :], 256)], ["P32", "ZZa", "ZZb"], ["pfz"], "pf", True)
            A(act(T.TS[:, 256 * t:256 * t + 256], zs, AF.Sigmoid, 0.0, 0.25), 256, ["pfz"], ["TS%d" % t], ["pf"])
            exchange(t, T.TS[:, 256 * t:256 * t + 256], T.TL[:, 256 * t:256 * t + 256], "at%d" % t, ["TS%d" % t], ["TL%d" % t], 4.0)
            A(act(T.UB[:, :], T.ZZ[:, :], AF.Sigmoid, 0.0, 0.25), 256, ["ZZa", "ZZb"], ["UB"])
            V(ts(Sall.indirect(T.LU[:, 48 * t + 16:48 * t + 32]), T.UB[:, :], 2.0, -1.0, ALU.mult, ALU.add), 256 * SCAT,
              ["UB", lu], ["S", "Sp0", "Sp1"])
            V(ts(Sall.indirect(T.LU[:, 48 * t:48 * t + 16]), T.TL[:, 256 * t:256 * t + 256], 2.0, -1.0, ALU.mult, ALU.add), 256 * SCAT,
              ["TL%d" % t, lu], ["S", "Sp0", "Sp1"])
        if PECH < NCH:
            A(act(T.OB[:, 256 * t + npe:256 * t + 256], so, AF.Identity), 256 - npe, sk, ["OBb%d" % t])
        dma("S", T.yo[:, 256 * t:256 * t + 256], T.OB[:, 256 * t:256 * t + 256], "outs", ["OBa%d" % t, "OBb%d" % t], (), 2.0, None)

    for t in range(RO):
        index_step(t)
        state_step(t)
    dma("S", T.yp[:, :], T.YP[0:128:16, :], "outs", ["YP0", "YP1"], (), 2.0, None)
    return nodes, sent[0]


def schedule(nodes):
    n = len(nodes)
    eng = [x["eng"] for x in nodes]
    deps = [list(x["deps"].items()) for x in nodes]
    succ = [[] for _ in range(n)]
    for i in range(n):
        for d, need in deps[i]:
            succ[d].append((i, need))
    costs = [[cost(x, m) for x in nodes] for m in MODELS]
    lats = [[x["lat"] * m[5] for x in nodes] for m in MODELS]
    c0, l0, hop0 = costs[0], lats[0], MODELS[0][4]
    base = [0.0] * n
    for i in range(n - 1, -1, -1):
        base[i] = c0[i] + l0[i] + hop0 + max([base[s] for s, need in succ[i]] + [0.0])

    def make(prio, delta):
        left = [len(d) for d in deps]
        ready = [0.0] * n
        pools = {e: [] for e in set(eng)}
        free = {e: 0.0 for e in pools}
        for i in range(n):
            if left[i] == 0:
                pools[eng[i]].append(i)
        order = []
        for _ in range(n):
            t0, e0 = 1e9, None
            for e, pool in pools.items():
                if pool:
                    st = max(min([ready[i] for i in pool]), free[e])
                    if st < t0 or (st == t0 and str(e) < str(e0)):
                        t0, e0 = st, e
            i = max(pools[e0], key=lambda i: prio[i] - delta * max(0.0, ready[i] - t0))
            pools[e0].remove(i)
            st = max(ready[i], free[e0])
            if e0 is not None:
                free[e0] = st + c0[i]
            done = st + c0[i] + l0[i]
            order.append(i)
            for s, need in succ[i]:
                ready[s] = max(ready[s], done + (hop0 if need else 0.0))
                left[s] -= 1
                if left[s] == 0:
                    pools[eng[s]].append(s)
        return order

    def ends(order, starts=None):
        out = []
        for k, m in enumerate(MODELS):
            c, l, hop = costs[k], lats[k], m[4]
            done, free = [0.0] * n, {}
            for i in order:
                st = free.get(eng[i], 0.0)
                for d, need in deps[i]:
                    r = done[d] + hop if need else done[d]
                    if r > st:
                        st = r
                if eng[i] is not None:
                    free[eng[i]] = st + c[i]
                done[i] = st + c[i] + l[i]
                if starts is not None and k == 0:
                    starts.append((i, st))
            out.append(max(done))
        return out

    seed = [12345]

    def rnd():
        seed[0] = (seed[0] * 1103515245 + 12345) % 2147483648
        return seed[0] / 2147483648.0
    best = None
    for delta in (1000.0, 300.0, 100.0, 50.0, 30.0, 20.0, 10.0, 5.0):
        order = make(base, delta)
        e = ends(order)
        if best is None:
            ref = e
        score = sum(WEIGHTS[k] * e[k] / ref[k] for k in range(len(e)))
        if best is None or score < best[0]:
            best = (score, order, list(base), delta)
    for r in range(ROUNDS):
        prio = list(best[2])
        for _ in range(1 + int(rnd() * MOVES)):
            prio[int(rnd() * n)] += (rnd() - 0.5) * STEP
        delta = best[3] if rnd() < 0.9 else best[3] * (0.5 + rnd())
        order = make(prio, delta)
        e = ends(order)
        score = sum(WEIGHTS[k] * e[k] / ref[k] for k in range(len(e)))
        if score <= best[0]:
            best = (score, order, prio, delta)
    starts = []
    return starts, ends(best[1], starts)


def rank_program(g, core, T, topo):
    rank = T.rank_of(core)
    if rank is None:
        return
    nodes, sent = build(g, core, T, topo, rank)
    if "order" not in ORDER:
        ORDER["order"] = schedule(nodes)[0]
    order = ORDER["order"]
    queue = {"P": g.tensor, "V": g.vector, "A": g.scalar, "G": g, "S": g.sync}
    signals = set()
    for x in nodes:
        if x["eng"] is not None:
            signals.update(d for d, need in x["deps"].items() if need)
    count, mark, seen = {}, {}, {}
    for i, st in order:
        x = nodes[i]
        e = x["eng"]
        if e is None:
            mark[i] = x["sem"]
            continue
        want = {}
        for d, need in x["deps"].items():
            if need:
                s, c = mark[d]
                want[s] = max(want.get(s, 0), c)
        for s, c in want.items():
            if seen.get((e, s), 0) < c:
                queue[e].wait_ge(T.sem[s], c)
                seen[(e, s)] = c
        ins = x["fn"]()
        if x["sem"] is not None:
            mark[i] = x["sem"]
        elif i in signals:
            s = "c" + e
            count[s] = count.get(s, 0) + 1
            ins.then_inc(T.sem[s], 1)
            mark[i] = (s, count[s])
    g.wait_ge(T.sem.sent, sent)
    g.sync.wait_ge(T.sem.outs, 16 * (RO + 1))
